import numpy as np, ml_dtypes
CORES = [52,68,84,180,196,212,308,324,340]
N = 9
import mx_ref
NC = 128
EPS = 0.001
BF = ml_dtypes.bfloat16
def setup_inputs(rng):
    def f(*shape):
        return mx_ref.flush((rng.standard_normal(shape, dtype=np.float32) * np.exp2(rng.integers(-2, 3, shape[:-1] + (1,)))).astype(BF))
    return {"x": f(N, 128, 512), "w": f(N, 128, 4 * NC)}
def setup_inputs_blocks(rng):
    d = setup_inputs(rng)
    for k in ("x", "w"): d[k] = mx_ref.spread(d[k], rng, 4)
    return d
def setup_inputs_wide(rng):
    d = setup_inputs(rng)
    for k in ("x", "w"): d[k] = mx_ref.flush((d[k].astype(np.float32) * np.exp2(rng.integers(-6, 7, (N, 1, 1))).astype(np.float32)).astype(BF))
    return d
def setup_inputs_tokens(rng):
    d = setup_inputs(rng); v = d["x"].astype(np.float32).reshape(N, 128, -1, 4)
    d["x"] = mx_ref.flush((v * np.exp2(rng.integers(-6, 7, (N, 1, v.shape[2], 1))).astype(np.float32)).reshape(d["x"].shape).astype(BF))
    return d
def setup_inputs_faint(rng):
    d = setup_inputs(rng); d["x"] = mx_ref.flush((d["x"].astype(np.float32) * np.float32(2.0 ** -12)).astype(BF))
    return d
def reference(x, w):
    W = [mx_ref.quantize(w[r]) for r in range(N)]
    y = np.zeros((N, 128, N * NC), np.float32)
    for j in range(N):
        X = mx_ref.quantize(x[j])
        Z = [mx_ref.matmul(X, W[r]) for r in range(N)]
        ms = sum((z.astype(np.float64) ** 2).sum(axis=1, keepdims=True) for z in Z) / (N * NC)
        for r in range(N):
            y[r][:, NC * j:NC * j + NC] = (Z[r] / np.sqrt(ms + EPS)).astype(np.float32)
    return {"y": y}

@@ -1,0 +1,313 @@
+import numpy as np
+import math
+from concourse.bass import DstId, RemoteDMATransfer
+from concourse.mybir import dt, AluOpType, AxisListType, ActivationFunctionType
+
+N = 9
+NC = 128
+EPS = 0.001
+WORLD = 512
+NSLOT = 12
+SW = 12
+
+SCRATCH = {
+    "xb": ("sbuf", [128, 512], "bfloat16"),
+    "wb": ("sbuf", [128, 512], "bfloat16"),
+    "q": ("sbuf", [128, NSLOT * NC], "float8_e4m3fn_x4"),
+    "sc": ("sbuf", [128, NSLOT * NC], "uint8"),
+    "zp": ("psum", [128, 4096], "float32"),
+    "ysb": ("sbuf", [128, N * NC], "float32"),
+    "junk": ("sbuf", [128, 3 * NC], "float32"),
+    "sp": ("sbuf", [128, SW], "float32"),
+    "sl": ("sbuf", [128, 3 * SW], "float32"),
+    "wk": ("sbuf", [128, 9 * SW], "float32"),
+}
+SEMAPHORES = ["ldx", "ldw", "qx", "qw", "mm", "sq", "ev", "S0", "S1", "vs", "sa", "zv", "zs", "st", "st2", "loc"] + [
+    "X%d" % j for j in range(N)]
+
+_CACHE = {}
+
+
+def _plan(T, topo):
+    if "p" in _CACHE:
+        return _CACHE["p"]
+    cores = [int(c) for c in T.cores]
+    hosts = sorted(set(topo.host(c) for c in cores))
+    ok = topo.may_write
+    hub_h = [h for h in hosts
+             if all(ok(a, b) and ok(b, a) for a in cores if topo.host(a) == h for b in cores if b != a)][0]
+    outer_h = [h for h in hosts if h != hub_h]
+    chips = sorted(set(topo.chip(c) for c in cores))
+    at = {(topo.host(c), topo.chip(c)): j for j, c in enumerate(cores)}
+
+    def rot(ch, d):
+        return chips[(chips.index(ch) + d) % len(chips)]
+
+    slot, order, role = {}, {}, {}
+    for j, c in enumerate(cores):
+        h, ch = topo.host(c), topo.chip(c)
+        m = {("W", j): 2}
+        if h == hub_h:
+            a, b = at[(outer_h[0], ch)], at[(outer_h[1], ch)]
+            m[("X", a)], m[("W", a)], m[("W", b)], m[("X", b)] = 0, 1, 3, 4
+            free = list(range(5, NSLOT))
+            m[("X", j)] = free.pop(0)
+            order[j] = [j, at[(h, rot(ch, -1))], at[(h, rot(ch, -2))], a, b,
+                        at[(outer_h[0], rot(ch, -1))], at[(outer_h[1], rot(ch, -1))],
+                        at[(outer_h[0], rot(ch, -2))], at[(outer_h[1], rot(ch, -2))]]
+        else:
+            if h == outer_h[0]:
+                m[("X", j)] = 1
+                free = [0] + list(range(3, NSLOT))
+            else:
+                m[("X", j)] = 3
+                free = [0, 1] + list(range(4, NSLOT))
+            o2 = [o for o in outer_h if o != h][0]
+            order[j] = [j, at[(hub_h, ch)], at[(hub_h, rot(ch, -1))], at[(hub_h, rot(ch, -2))],
+                        at[(o2, ch)], at[(h, rot(ch, -1))], at[(o2, rot(ch, -1))],
+                        at[(h, rot(ch, -2))], at[(o2, rot(ch, -2))]]
+        for i in range(N):
+            if ("X", i) not in m:
+                m[("X", i)] = free.pop(0)
+        slot[j] = m
+    relay, helpers = {}, {}
+    for j, c in enumerate(cores):
+        h, ch = topo.host(c), topo.chip(c)
+        if h == hub_h:
+            sib = [k for k in range(WORLD) if k != c and topo.host(k) == h and topo.chip(k) == ch
+                   and topo.die(k) == topo.die(c)]
+            helpers[j] = (sib[0], sib[-1])
+            for k, o in zip(helpers[j], outer_h):
+                role[k] = (j, [at[(o, rot(ch, 1))], at[(o, rot(ch, 2))]])
+        else:
+            far = [d for d in cores if d != c and not ok(c, d)]
+            cand = [k for k in range(WORLD) if topo.host(k) not in hosts and topo.chip(k) == ch
+                    and topo.die(k) == topo.die(c) and ok(c, k) and all(ok(k, d) for d in far)]
+            relay[j] = cand[0] if h == outer_h[0] else cand[-1]
+            fh = topo.host(far[0])
+            role[relay[j]] = (j, [at[(fh, ch)], at[(fh, rot(ch, 1))], at[(fh, rot(ch, 2))]])
+    groups = [[j for j, c in enumerate(cores) if topo.host(c) == h] for h in [hub_h] + outer_h]
+    p = dict(cores=cores, hub_h=hub_h, outer_h=outer_h, at=at, rot=rot, slot=slot, order=order, role=role,
+             relay=relay, helpers=helpers, groups=groups)
+    _CACHE["p"] = p
+    return p
+
+
+def _ne(mask):
+    return bin(mask).count("1")
+
+
+def _write(g, T, topo, core, dsts, src, outs, sem, mask, tot):
+    ids = [topo.addr(d, core) for d in dsts]
+    if len(dsts) == 1:
+        g.remote_dma(outs[0], src, sem, T.sem.loc, ids[0][1], ids[0][0], mask)
+    else:
+        g.remote_dma_fused([RemoteDMATransfer(dst_ids=[DstId(rid=r, pnc=p) for r, p in ids], dma_engine_mask=mask,
+                                              remote_sem=sem, srcs=[src], dsts=outs)], local_sem=T.sem.loc)
+    tot["loc"] = tot.get("loc", 0) + _ne(mask)
+
+
+def _tiles(g, T, topo, core, dsts, s0, d0s, ns, sem, mask, tot):
+    _write(g, T, topo, core, dsts, T.q[:, s0 * NC:(s0 + ns) * NC].bitcast(dt.uint8),
+           [T.q[:, d * NC:(d + ns) * NC].bitcast(dt.uint8) for d in d0s], sem, mask, tot)
+    _write(g, T, topo, core, dsts, T.sc[:, s0 * NC:(s0 + ns) * NC],
+           [T.sc[:, d * NC:(d + ns) * NC] for d in d0s], sem, mask, tot)
+
+
+def rank_program(g, core, T, topo):
+    P = _plan(T, topo)
+    cores, slot, at, rot = P["cores"], P["slot"], P["at"], P["rot"]
+    S = T.sem
+    tot = {}
+    me = T.rank_of(core)
+    if me is None:
+        if core not in P["role"]:
+            return
+        j, ds = P["role"][core]
+        g.wait_ge(S["X%d" % j], 16)
+        _tiles(g, T, topo, core, [cores[d] for d in ds], 0, [slot[d][("X", j)] for d in ds], 1, S["X%d" % j],
+               topo.mask(core, cores[ds[0]]), tot)
+        g.wait_ge(S.loc, tot["loc"])
+        return
+
+    V, A, TE, SY = g.vector, g.scalar, g.tensor, g.sync
+    MUL, ADD = AluOpType.mult, AluOpType.add
+    h, ch = topo.host(core), topo.chip(core)
+    hub = h == P["hub_h"]
+    sl_me = slot[me]
+    xs = sl_me[("X", me)]
+    order = P["order"][me]
+    pos = {j: k for k, j in enumerate(order)}
+    hubs = P["groups"][0]
+    batches = [P["groups"][0], P["groups"][1] + P["groups"][2]]
+    lo = [0, 4]
+    col = {}
+    for b, js in enumerate(batches):
+        for i, j in enumerate(js):
+            col[j] = lo[b] + i
+    semx = lambda j: S["X%d" % j]
+
+    SY.dma_start(T.xb[:], T.x[:]).then_inc(S.ldx, 16)
+    A.dma_start(T.wb[:], T.w[:]).then_inc(S.ldw, 16)
+    V.wait_ge(S.ldx, 16)
+    V.quantize_mx(T.q[:, xs * NC:(xs + 1) * NC], T.sc[:, xs * NC:(xs + 1) * NC], T.xb[:]).then_inc(S.qx, 1)
+    V.wait_ge(S.ldw, 16)
+    V.quantize_mx(T.q[:, 2 * NC:3 * NC], T.sc[:, 2 * NC:3 * NC], T.wb[:]).then_inc(S.qw, 1)
+    tot.update(ldx=16, ldw=16, qx=1, qw=1)
+
+    def xto(ds, mask):
+        _tiles(g, T, topo, core, [cores[d] for d in ds], xs, [slot[d][("X", me)] for d in ds], 1, semx(me), mask, tot)
+
+    g.wait_ge(S.qx, 1)
+    if hub:
+        partners = [at[(o, ch)] for o in P["outer_h"]]
+        peers = [at[(h, rot(ch, 1))], at[(h, rot(ch, 2))]]
+        off = topo.mask(core, cores[peers[0]])
+        hs = list(P["helpers"][me])
+        _tiles(g, T, topo, core, hs, xs, [0, 0], 1, semx(me), topo.mask(core, hs[0]) & ~off, tot)
+        xto(peers, off)
+        xto(partners, off)
+    else:
+        partner = at[(P["hub_h"], ch)]
+        off = topo.mask(core, cores[partner])
+        rl = P["relay"][me]
+        _tiles(g, T, topo, core, [rl], xs, [0], 1, semx(me), topo.mask(core, rl), tot)
+        g.wait_ge(S.qw, 1)
+        s0 = min(xs, 2)
+        d0 = min(slot[partner][("X", me)], slot[partner][("W", me)])
+        _tiles(g, T, topo, core, [cores[partner]], s0, [d0], 2, semx(me), off, tot)
+        xto([at[(P["hub_h"], rot(ch, 1))], at[(P["hub_h"], rot(ch, 2))]], off)
+        xto([at[(h, rot(ch, 1))], at[(h, rot(ch, 2))]], off)
+    for j in range(N):
+        if j != me:
+            tot["X%d" % j] = 16
+
+    w0, nw, own = (1, 3, NC) if hub else (2, 1, 0)
+    TE.wait_ge(S.qx, 1)
+    TE.wait_ge(S.qw, 1)
+    if hub:
+        for j in partners:
+            TE.wait_ge(semx(j), 16)
+    for k, j in enumerate(order):
+        if j != me and not (hub and j in partners):
+            TE.wait_ge(semx(j), 16)
+        if k >= 8:
+            TE.wait_ge(S.ev, 1)
+        s = sl_me[("X", j)]
+        bk = (k % 8) * 512
+        TE.matmul_mx(T.zp[:, bk:bk + nw * NC], T.q[:, s * NC:(s + 1) * NC], T.sc[:, s * NC:(s + 1) * NC],
+                     T.q[:, w0 * NC:(w0 + nw) * NC], T.sc[:, w0 * NC:(w0 + nw) * NC], True, True).then_inc(S.mm, 1)
+    tot["mm"] = N
+
+    def zsrc(j):
+        k = pos[j]
+        if k == 0:
+            return T.ysb[:, j * NC:(j + 1) * NC]
+        bk = (k % 8) * 512 + own
+        return T.zp[:, bk:bk + NC]
+
+    if hub:
+        for k, j in enumerate(order):
+            A.wait_ge(S.mm, k + 1)
+            if k:
+                A.wait_ge(S.sq, k)
+            bk = (k % 8) * 512
+            A.activation(T.junk[:], T.zp[:, bk:bk + nw * NC], ActivationFunctionType.Square,
+                         accum_out=T.sp[:, col[j]:col[j] + 1]).then_inc(S.sq, 1)
+        tot["sq"] = N
+        hi = hubs.index(me)
+        others = [d for d in range(N) if d != me]
+        others = others[3 * hi % 8:] + others[:3 * hi % 8]
+        done = 0
+        for b, js in enumerate(batches):
+            done += len(js)
+            g.wait_ge(S.sq, done)
+            a0, a1 = lo[b], lo[b] + len(js)
+            _write(g, T, topo, core, [cores[d] for d in others], T.sp[:, a0:a1],
+                   [T.sl[:, hi * SW + a0:hi * SW + a1] for d in others], S["S%d" % b], off, tot)
+        V.wait_ge(S.sq, 1)
+    else:
+        V.wait_ge(S.mm, 1)
+    V.tensor_copy(T.ysb[:, me * NC:(me + 1) * NC], T.zp[:, own:own + NC]).then_inc(S.ev, 1)
+    tot["ev"] = 1
+
+    c = {"vs": 0, "sa": 0, "zv": 0, "zs": 0, "st": 0, "st2": 0}
+
+    def vop(inst):
+        inst.then_inc(S.vs, 1)
+        c["vs"] += 1
+
+    def vsync():
+        V.wait_ge(S.vs, c["vs"])
+
+    def scale(eng, j):
+        q = V if eng == "v" else A
+        if pos[j] == 0:
+            q.wait_ge(S.ev, 1)
+        else:
+            q.wait_ge(S.mm, pos[j] + 1)
+        out = T.ysb[:, j * NC:(j + 1) * NC]
+        rc = T.wk[:, 8 * SW + col[j]:8 * SW + col[j] + 1]
+        if eng == "v":
+            V.tensor_scalar(out, zsrc(j), rc, None, MUL).then_inc(S.zv, 1)
+            c["zv"] += 1
+        else:
+            A.activation(out, zsrc(j), ActivationFunctionType.Copy, scale=rc).then_inc(S.zs, 1)
+            c["zs"] += 1
+
+    nrem = len([d for d in hubs if d != me])
+    inv = 1.0 / (N * NC)
+    done = 0
+    for b, js in enumerate(batches):
+        done += len(js)
+        a0, a1 = lo[b], lo[b] + len(js)
+        R = lambda k: T.wk[:, k * SW + a0:k * SW + a1]
+        parts = [T.sp[:, a0:a1] if d == me else T.sl[:, i * SW + a0:i * SW + a1] for i, d in enumerate(hubs)]
+        V.wait_ge(S["S%d" % b], 8 * nrem)
+        tot["S%d" % b] = 8 * nrem
+        if hub:
+            V.wait_ge(S.sq, done)
+        vop(V.tensor_tensor(R(0), parts[0], parts[1], ADD))
+        vsync()
+        vop(V.tensor_tensor(R(1), R(0), parts[2], ADD))
+        A.wait_ge(S.vs, c["vs"])
+        A.activation(R(3), R(1), ActivationFunctionType.Sqrt, bias=EPS, scale=inv).then_inc(S.sa, 1)
+        c["sa"] += 1
+        vsync()
+        vop(V.tensor_scalar(R(2), R(1), inv, EPS, MUL, ADD))
+        V.wait_ge(S.sa, c["sa"])
+        vop(V.reciprocal(R(4), R(3)))
+        vsync()
+        vop(V.tensor_tensor(R(5), R(2), R(4), MUL))
+        vsync()
+        vop(V.tensor_tensor(R(6), R(5), R(4), MUL))
+        vsync()
+        vop(V.tensor_scalar(R(7), R(6), -0.5, 1.5, MUL, ADD))
+        vsync()
+        vop(V.tensor_tensor(R(8), R(4), R(7), MUL))
+        vsync()
+        A.wait_ge(S.vs, c["vs"])
+        if b == 0:
+            scale("v", js[0])
+            scale("s", js[2])
+            scale("v", js[1])
+            SY.wait_ge(S.zv, c["zv"])
+            SY.wait_ge(S.zs, c["zs"])
+            SY.dma_start(T.y[:, js[0] * NC:(js[-1] + 1) * NC], T.ysb[:, js[0] * NC:(js[-1] + 1) * NC]).then_inc(S.st, 16)
+            c["st"] += 16
+        else:
+            ga, gb = P["groups"][1], P["groups"][2]
+            for j in ga:
+                scale("v", j)
+            for j in gb:
+                scale("s", j)
+            SY.wait_ge(S.zv, c["zv"])
+            SY.dma_start(T.y[:, ga[0] * NC:(ga[-1] + 1) * NC], T.ysb[:, ga[0] * NC:(ga[-1] + 1) * NC]).then_inc(S.st, 16)
+            c["st"] += 16
+            A.wait_ge(S.zs, c["zs"])
+            A.dma_start(T.y[:, gb[0] * NC:(gb[-1] + 1) * NC], T.ysb[:, gb[0] * NC:(gb[-1] + 1) * NC]).then_inc(S.st2, 16)
+            c["st2"] += 16
+    tot.update(c)
+
+    for name in sorted(tot, key=lambda n: n in ("st", "st2")):
+        g.wait_ge(S[name], tot[name])

@@ -9,6 +9,7 @@ EPS = 0.001
 WORLD = 512
 NSLOT = 12
 SW = 12
+LO = [0, 4]
 
 SCRATCH = {
     "xb": ("sbuf", [128, 512], "bfloat16"),
@@ -28,6 +29,10 @@ SEMAPHORES = ["ldx", "ldw", "qx", "qw", "mm", "sq", "ev", "S0", "S1", "vs", "sa"
 _CACHE = {}
 
 
+def _ne(mask):
+    return bin(mask).count("1")
+
+
 def _plan(T, topo):
     if "p" in _CACHE:
         return _CACHE["p"]
@@ -43,7 +48,7 @@ def _plan(T, topo):
     def rot(ch, d):
         return chips[(chips.index(ch) + d) % len(chips)]
 
-    slot, order, role = {}, {}, {}
+    slot, order = {}, {}
     for j, c in enumerate(cores):
         h, ch = topo.host(c), topo.chip(c)
         m = {("W", j): 2}
@@ -70,31 +75,44 @@ def _plan(T, topo):
             if ("X", i) not in m:
                 m[("X", i)] = free.pop(0)
         slot[j] = m
-    relay, helpers = {}, {}
+
+    fwd, sumh, hand = {}, {}, {}
     for j, c in enumerate(cores):
         h, ch = topo.host(c), topo.chip(c)
+        mates = [k for k in range(WORLD) if k != c and topo.host(k) == h and topo.chip(k) == ch]
+        same = [k for k in mates if topo.die(k) == topo.die(c)]
+        oth = [k for k in mates if topo.die(k) != topo.die(c)]
         if h == hub_h:
-            sib = [k for k in range(WORLD) if k != c and topo.host(k) == h and topo.chip(k) == ch
-                   and topo.die(k) == topo.die(c)]
-            helpers[j] = (sib[0], sib[-1])
-            for k, o in zip(helpers[j], outer_h):
-                role[k] = (j, [at[(o, rot(ch, 1))], at[(o, rot(ch, 2))]])
+            off = topo.mask(c, cores[at[(h, rot(ch, 1))]])
+            up = topo.mask(c, oth[0]) & ~off
+            hq, hs = (oth[1], oth[0]), oth[-1]
+            for k, o in zip(hq, outer_h):
+                fwd[k] = (j, "q", _ne(up), [[at[(o, rot(ch, d))] for d in (0, 1, 2)]])
+            fwd[hs] = (j, "s", _ne(up), [[at[(o, rot(ch, d))] for d in (0, 1, 2) for o in outer_h]])
+            sm = (same[0], same[-1])
+            for k, o in zip(sm, outer_h):
+                sumh[k] = (j, _ne(up), [at[(o, rot(ch, 1))], at[(o, rot(ch, 2))]])
+            hand[j] = dict(off=off, up=up, hq=hq, hs=hs, sm=sm)
         else:
+            off = topo.mask(c, cores[at[(hub_h, ch)]])
+            up = topo.mask(c, oth[0]) & ~off
+            calls = [[at[(hub_h, rot(ch, 1))], at[(hub_h, rot(ch, 2))]], [at[(h, rot(ch, 1))], at[(h, rot(ch, 2))]]]
+            fwd[oth[0]] = (j, "q", _ne(up), calls)
+            fwd[oth[-1]] = (j, "s", _ne(up), calls)
             far = [d for d in cores if d != c and not ok(c, d)]
             cand = [k for k in range(WORLD) if topo.host(k) not in hosts and topo.chip(k) == ch
                     and topo.die(k) == topo.die(c) and ok(c, k) and all(ok(k, d) for d in far)]
-            relay[j] = cand[0] if h == outer_h[0] else cand[-1]
+            rq, rs = (cand[0], cand[2]) if h == outer_h[0] else (cand[-1], cand[1])
             fh = topo.host(far[0])
-            role[relay[j]] = (j, [at[(fh, ch)], at[(fh, rot(ch, 1))], at[(fh, rot(ch, 2))]])
+            fd = [[at[(fh, rot(ch, d))] for d in (0, 1, 2)]]
+            fwd[rq] = (j, "q", _ne(topo.mask(c, rq)), fd)
+            fwd[rs] = (j, "s", _ne(topo.mask(c, rs)), fd)
+            hand[j] = dict(off=off, up=up, hq=oth[0], hs=oth[-1], rq=rq, rs=rs)
     groups = [[j for j, c in enumerate(cores) if topo.host(c) == h] for h in [hub_h] + outer_h]
-    p = dict(cores=cores, hub_h=hub_h, outer_h=outer_h, at=at, rot=rot, slot=slot, order=order, role=role,
-             relay=relay, helpers=helpers, groups=groups)
+    p = dict(cores=cores, hub_h=hub_h, outer_h=outer_h, at=at, rot=rot, slot=slot, order=order, fwd=fwd, sumh=sumh,
+             hand=hand, groups=groups)
     _CACHE["p"] = p
     return p
-
-
-def _ne(mask):
-    return bin(mask).count("1")
 
 
 def _write(g, T, topo, core, dsts, src, outs, sem, mask, tot):
@@ -107,11 +125,10 @@ def _write(g, T, topo, core, dsts, src, outs, sem, mask, tot):
     tot["loc"] = tot.get("loc", 0) + _ne(mask)
 
 
-def _tiles(g, T, topo, core, dsts, s0, d0s, ns, sem, mask, tot):
-    _write(g, T, topo, core, dsts, T.q[:, s0 * NC:(s0 + ns) * NC].bitcast(dt.uint8),
-           [T.q[:, d * NC:(d + ns) * NC].bitcast(dt.uint8) for d in d0s], sem, mask, tot)
-    _write(g, T, topo, core, dsts, T.sc[:, s0 * NC:(s0 + ns) * NC],
-           [T.sc[:, d * NC:(d + ns) * NC] for d in d0s], sem, mask, tot)
+def _piece(T, kind, s, ns):
+    if kind == "q":
+        return T.q[:, s * NC:(s + ns) * NC].bitcast(dt.uint8)
+    return T.sc[:, s * NC:(s + ns) * NC]
 
 
 def rank_program(g, core, T, topo):
@@ -120,14 +137,27 @@ def rank_program(g, core, T, topo):
     S = T.sem
     tot = {}
     me = T.rank_of(core)
+    hubs = P["groups"][0]
+    batches = [P["groups"][0], P["groups"][1] + P["groups"][2]]
     if me is None:
-        if core not in P["role"]:
-            return
-        j, ds = P["role"][core]
-        g.wait_ge(S["X%d" % j], 16)
-        _tiles(g, T, topo, core, [cores[d] for d in ds], 0, [slot[d][("X", j)] for d in ds], 1, S["X%d" % j],
-               topo.mask(core, cores[ds[0]]), tot)
-        g.wait_ge(S.loc, tot["loc"])
+        if core in P["fwd"]:
+            j, kind, nin, calls = P["fwd"][core]
+            g.wait_ge(S["X%d" % j], nin)
+            for ds in calls:
+                _write(g, T, topo, core, [cores[d] for d in ds], _piece(T, kind, 0, 1),
+                       [_piece(T, kind, slot[d][("X", j)], 1) for d in ds], S["X%d" % j],
+                       topo.mask(core, cores[ds[0]]), tot)
+            g.wait_ge(S.loc, tot["loc"])
+        elif core in P["sumh"]:
+            j, nin, ds = P["sumh"][core]
+            hi = hubs.index(j)
+            for b, js in enumerate(batches):
+                a0, a1 = LO[b], LO[b] + len(js)
+                g.wait_ge(S["S%d" % b], nin)
+                _write(g, T, topo, core, [cores[d] for d in ds], T.sp[:, a0:a1],
+                       [T.sl[:, hi * SW + a0:hi * SW + a1] for d in ds], S["S%d" % b],
+                       topo.mask(core, cores[ds[0]]), tot)
+            g.wait_ge(S.loc, tot["loc"])
         return
 
     V, A, TE, SY = g.vector, g.scalar, g.tensor, g.sync
@@ -138,13 +168,12 @@ def rank_program(g, core, T, topo):
     xs = sl_me[("X", me)]
     order = P["order"][me]
     pos = {j: k for k, j in enumerate(order)}
-    hubs = P["groups"][0]
-    batches = [P["groups"][0], P["groups"][1] + P["groups"][2]]
-    lo = [0, 4]
+    H = P["hand"][me]
+    off, up = H["off"], H["up"]
     col = {}
     for b, js in enumerate(batches):
         for i, j in enumerate(js):
-            col[j] = lo[b] + i
+            col[j] = LO[b] + i
     semx = lambda j: S["X%d" % j]
 
     SY.dma_start(T.xb[:], T.x[:]).then_inc(S.ldx, 16)
@@ -155,42 +184,43 @@ def rank_program(g, core, T, topo):
     V.quantize_mx(T.q[:, 2 * NC:3 * NC], T.sc[:, 2 * NC:3 * NC], T.wb[:]).then_inc(S.qw, 1)
     tot.update(ldx=16, ldw=16, qx=1, qw=1)
 
-    def xto(ds, mask):
-        _tiles(g, T, topo, core, [cores[d] for d in ds], xs, [slot[d][("X", me)] for d in ds], 1, semx(me), mask, tot)
+    def put(kind, dsts, s0, d0s, ns, mask):
+        _write(g, T, topo, core, dsts, _piece(T, kind, s0, ns), [_piece(T, kind, d, ns) for d in d0s], semx(me),
+               mask, tot)
 
     g.wait_ge(S.qx, 1)
     if hub:
         partners = [at[(o, ch)] for o in P["outer_h"]]
         peers = [at[(h, rot(ch, 1))], at[(h, rot(ch, 2))]]
-        off = topo.mask(core, cores[peers[0]])
-        hs = list(P["helpers"][me])
-        _tiles(g, T, topo, core, hs, xs, [0, 0], 1, semx(me), topo.mask(core, hs[0]) & ~off, tot)
-        xto(peers, off)
-        xto(partners, off)
+        for kind in "qs":
+            put(kind, [cores[d] for d in peers], xs, [slot[d][("X", me)] for d in peers], 1, off)
+        put("q", list(H["hq"]), xs, [0, 0], 1, up)
+        put("s", [H["hs"]], xs, [0], 1, up)
     else:
         partner = at[(P["hub_h"], ch)]
-        off = topo.mask(core, cores[partner])
-        rl = P["relay"][me]
-        _tiles(g, T, topo, core, [rl], xs, [0], 1, semx(me), topo.mask(core, rl), tot)
+        put("q", [H["hq"]], xs, [0], 1, up)
+        put("s", [H["hs"]], xs, [0], 1, up)
         g.wait_ge(S.qw, 1)
         s0 = min(xs, 2)
         d0 = min(slot[partner][("X", me)], slot[partner][("W", me)])
-        _tiles(g, T, topo, core, [cores[partner]], s0, [d0], 2, semx(me), off, tot)
-        xto([at[(P["hub_h"], rot(ch, 1))], at[(P["hub_h"], rot(ch, 2))]], off)
-        xto([at[(h, rot(ch, 1))], at[(h, rot(ch, 2))]], off)
+        for kind in "qs":
+            put(kind, [cores[partner]], s0, [d0], 2, off)
+        put("q", [H["rq"]], xs, [0], 1, topo.mask(core, H["rq"]))
+        put("s", [H["rs"]], xs, [0], 1, topo.mask(core, H["rs"]))
+    nx = 2 * _ne(off)
     for j in range(N):
         if j != me:
-            tot["X%d" % j] = 16
+            tot["X%d" % j] = nx
 
     w0, nw, own = (1, 3, NC) if hub else (2, 1, 0)
     TE.wait_ge(S.qx, 1)
     TE.wait_ge(S.qw, 1)
     if hub:
         for j in partners:
-            TE.wait_ge(semx(j), 16)
+            TE.wait_ge(semx(j), nx)
     for k, j in enumerate(order):
         if j != me and not (hub and j in partners):
-            TE.wait_ge(semx(j), 16)
+            TE.wait_ge(semx(j), nx)
         if k >= 8:
             TE.wait_ge(S.ev, 1)
         s = sl_me[("X", j)]
@@ -216,15 +246,16 @@ def rank_program(g, core, T, topo):
                          accum_out=T.sp[:, col[j]:col[j] + 1]).then_inc(S.sq, 1)
         tot["sq"] = N
         hi = hubs.index(me)
-        others = [d for d in range(N) if d != me]
-        others = others[3 * hi % 8:] + others[:3 * hi % 8]
+        direct = peers + partners
         done = 0
         for b, js in enumerate(batches):
             done += len(js)
             g.wait_ge(S.sq, done)
-            a0, a1 = lo[b], lo[b] + len(js)
-            _write(g, T, topo, core, [cores[d] for d in others], T.sp[:, a0:a1],
-                   [T.sl[:, hi * SW + a0:hi * SW + a1] for d in others], S["S%d" % b], off, tot)
+            a0, a1 = LO[b], LO[b] + len(js)
+            _write(g, T, topo, core, list(H["sm"]), T.sp[:, a0:a1], [T.sp[:, a0:a1] for d in H["sm"]],
+                   S["S%d" % b], up, tot)
+            _write(g, T, topo, core, [cores[d] for d in direct], T.sp[:, a0:a1],
+                   [T.sl[:, hi * SW + a0:hi * SW + a1] for d in direct], S["S%d" % b], off, tot)
         V.wait_ge(S.sq, 1)
     else:
         V.wait_ge(S.mm, 1)
@@ -260,11 +291,11 @@ def rank_program(g, core, T, topo):
     done = 0
     for b, js in enumerate(batches):
         done += len(js)
-        a0, a1 = lo[b], lo[b] + len(js)
+        a0, a1 = LO[b], LO[b] + len(js)
         R = lambda k: T.wk[:, k * SW + a0:k * SW + a1]
         parts = [T.sp[:, a0:a1] if d == me else T.sl[:, i * SW + a0:i * SW + a1] for i, d in enumerate(hubs)]
-        V.wait_ge(S["S%d" % b], 8 * nrem)
-        tot["S%d" % b] = 8 * nrem
+        V.wait_ge(S["S%d" % b], _ne(off) * nrem)
+        tot["S%d" % b] = _ne(off) * nrem
         if hub:
             V.wait_ge(S.sq, done)
         vop(V.tensor_tensor(R(0), parts[0], parts[1], ADD))

import numpy as np
import math
from concourse.bass import DstId, RemoteDMATransfer
from concourse.mybir import dt, AluOpType, AxisListType, ActivationFunctionType

N = 9
NC = 128
EPS = 0.001
WORLD = 512
NSLOT = 12
SW = 12
LO = [0, 4]

SCRATCH = {
    "xb": ("sbuf", [128, 512], "bfloat16"),
    "wb": ("sbuf", [128, 512], "bfloat16"),
    "q": ("sbuf", [128, NSLOT * NC], "float8_e4m3fn_x4"),
    "sc": ("sbuf", [128, NSLOT * NC], "uint8"),
    "zp": ("psum", [128, 4096], "float32"),
    "ysb": ("sbuf", [128, N * NC], "float32"),
    "junk": ("sbuf", [128, 3 * NC], "float32"),
    "sp": ("sbuf", [128, SW], "float32"),
    "sl": ("sbuf", [128, 3 * SW], "float32"),
    "wk": ("sbuf", [128, 9 * SW], "float32"),
}
SEMAPHORES = ["ldx", "ldw", "qx", "qw", "mm", "sq", "ev", "S0", "S1", "vs", "sa", "zv", "zs", "st", "st2", "loc"] + [
    "X%d" % j for j in range(N)]

_CACHE = {}


def _ne(mask):
    return bin(mask).count("1")


def _plan(T, topo):
    if "p" in _CACHE:
        return _CACHE["p"]
    cores = [int(c) for c in T.cores]
    hosts = sorted(set(topo.host(c) for c in cores))
    ok = topo.may_write
    hub_h = [h for h in hosts
             if all(ok(a, b) and ok(b, a) for a in cores if topo.host(a) == h for b in cores if b != a)][0]
    outer_h = [h for h in hosts if h != hub_h]
    chips = sorted(set(topo.chip(c) for c in cores))
    at = {(topo.host(c), topo.chip(c)): j for j, c in enumerate(cores)}

    def rot(ch, d):
        return chips[(chips.index(ch) + d) % len(chips)]

    slot, order = {}, {}
    for j, c in enumerate(cores):
        h, ch = topo.host(c), topo.chip(c)
        m = {("W", j): 2}
        if h == hub_h:
            a, b = at[(outer_h[0], ch)], at[(outer_h[1], ch)]
            m[("X", a)], m[("W", a)], m[("W", b)], m[("X", b)] = 0, 1, 3, 4
            free = list(range(5, NSLOT))
            m[("X", j)] = free.pop(0)
            order[j] = [j, at[(h, rot(ch, -1))], at[(h, rot(ch, -2))], a, b,
                        at[(outer_h[0], rot(ch, -1))], at[(outer_h[1], rot(ch, -1))],
                        at[(outer_h[0], rot(ch, -2))], at[(outer_h[1], rot(ch, -2))]]
        else:
            if h == outer_h[0]:
                m[("X", j)] = 1
                free = [0] + list(range(3, NSLOT))
            else:
                m[("X", j)] = 3
                free = [0, 1] + list(range(4, NSLOT))
            o2 = [o for o in outer_h if o != h][0]
            order[j] = [j, at[(hub_h, ch)], at[(hub_h, rot(ch, -1))], at[(hub_h, rot(ch, -2))],
                        at[(o2, ch)], at[(h, rot(ch, -1))], at[(o2, rot(ch, -1))],
                        at[(h, rot(ch, -2))], at[(o2, rot(ch, -2))]]
        for i in range(N):
            if ("X", i) not in m:
                m[("X", i)] = free.pop(0)
        slot[j] = m

    fwd, sumh, hand = {}, {}, {}
    for j, c in enumerate(cores):
        h, ch = topo.host(c), topo.chip(c)
        mates = [k for k in range(WORLD) if k != c and topo.host(k) == h and topo.chip(k) == ch]
        same = [k for k in mates if topo.die(k) == topo.die(c)]
        oth = [k for k in mates if topo.die(k) != topo.die(c)]
        if h == hub_h:
            off = topo.mask(c, cores[at[(h, rot(ch, 1))]])
            up = topo.mask(c, oth[0]) & ~off
            hq, hs = (oth[1], oth[0]), oth[-1]
            for k, o in zip(hq, outer_h):
                fwd[k] = (j, "q", _ne(up), [[at[(o, rot(ch, d))] for d in (0, 1, 2)]])
            fwd[hs] = (j, "s", _ne(up), [[at[(o, rot(ch, d))] for d in (0, 1, 2) for o in outer_h]])
            sm = (same[0], same[-1])
            for k, o in zip(sm, outer_h):
                sumh[k] = (j, _ne(up), [at[(o, rot(ch, 1))], at[(o, rot(ch, 2))]])
            hand[j] = dict(off=off, up=up, hq=hq, hs=hs, sm=sm)
        else:
            off = topo.mask(c, cores[at[(hub_h, ch)]])
            up = topo.mask(c, oth[0]) & ~off
            calls = [[at[(hub_h, rot(ch, 1))], at[(hub_h, rot(ch, 2))]], [at[(h, rot(ch, 1))], at[(h, rot(ch, 2))]]]
            fwd[oth[0]] = (j, "q", _ne(up), calls)
            fwd[oth[-1]] = (j, "s", _ne(up), calls)
            far = [d for d in cores if d != c and not ok(c, d)]
            cand = [k for k in range(WORLD) if topo.host(k) not in hosts and topo.chip(k) == ch
                    and topo.die(k) == topo.die(c) and ok(c, k) and all(ok(k, d) for d in far)]
            rq, rs = (cand[0], cand[2]) if h == outer_h[0] else (cand[-1], cand[1])
            fh = topo.host(far[0])
            fd = [[at[(fh, rot(ch, d))] for d in (0, 1, 2)]]
            fwd[rq] = (j, "q", _ne(topo.mask(c, rq)), fd)
            fwd[rs] = (j, "s", _ne(topo.mask(c, rs)), fd)
            hand[j] = dict(off=off, up=up, hq=oth[0], hs=oth[-1], rq=rq, rs=rs)
    groups = [[j for j, c in enumerate(cores) if topo.host(c) == h] for h in [hub_h] + outer_h]
    p = dict(cores=cores, hub_h=hub_h, outer_h=outer_h, at=at, rot=rot, slot=slot, order=order, fwd=fwd, sumh=sumh,
             hand=hand, groups=groups)
    _CACHE["p"] = p
    return p


def _write(g, T, topo, core, dsts, src, outs, sem, mask, tot):
    ids = [topo.addr(d, core) for d in dsts]
    if len(dsts) == 1:
        g.remote_dma(outs[0], src, sem, T.sem.loc, ids[0][1], ids[0][0], mask)
    else:
        g.remote_dma_fused([RemoteDMATransfer(dst_ids=[DstId(rid=r, pnc=p) for r, p in ids], dma_engine_mask=mask,
                                              remote_sem=sem, srcs=[src], dsts=outs)], local_sem=T.sem.loc)
    tot["loc"] = tot.get("loc", 0) + _ne(mask)


def _piece(T, kind, s, ns):
    if kind == "q":
        return T.q[:, s * NC:(s + ns) * NC].bitcast(dt.uint8)
    return T.sc[:, s * NC:(s + ns) * NC]


def rank_program(g, core, T, topo):
    P = _plan(T, topo)
    cores, slot, at, rot = P["cores"], P["slot"], P["at"], P["rot"]
    S = T.sem
    tot = {}
    me = T.rank_of(core)
    hubs = P["groups"][0]
    batches = [P["groups"][0], P["groups"][1] + P["groups"][2]]
    if me is None:
        if core in P["fwd"]:
            j, kind, nin, calls = P["fwd"][core]
            g.wait_ge(S["X%d" % j], nin)
            for ds in calls:
                _write(g, T, topo, core, [cores[d] for d in ds], _piece(T, kind, 0, 1),
                       [_piece(T, kind, slot[d][("X", j)], 1) for d in ds], S["X%d" % j],
                       topo.mask(core, cores[ds[0]]), tot)
            g.wait_ge(S.loc, tot["loc"])
        elif core in P["sumh"]:
            j, nin, ds = P["sumh"][core]
            hi = hubs.index(j)
            for b, js in enumerate(batches):
                a0, a1 = LO[b], LO[b] + len(js)
                g.wait_ge(S["S%d" % b], nin)
                _write(g, T, topo, core, [cores[d] for d in ds], T.sp[:, a0:a1],
                       [T.sl[:, hi * SW + a0:hi * SW + a1] for d in ds], S["S%d" % b],
                       topo.mask(core, cores[ds[0]]), tot)
            g.wait_ge(S.loc, tot["loc"])
        return

    V, A, TE, SY = g.vector, g.scalar, g.tensor, g.sync
    MUL, ADD = AluOpType.mult, AluOpType.add
    h, ch = topo.host(core), topo.chip(core)
    hub = h == P["hub_h"]
    sl_me = slot[me]
    xs = sl_me[("X", me)]
    order = P["order"][me]
    pos = {j: k for k, j in enumerate(order)}
    H = P["hand"][me]
    off, up = H["off"], H["up"]
    col = {}
    for b, js in enumerate(batches):
        for i, j in enumerate(js):
            col[j] = LO[b] + i
    semx = lambda j: S["X%d" % j]

    SY.dma_start(T.xb[:], T.x[:]).then_inc(S.ldx, 16)
    A.dma_start(T.wb[:], T.w[:]).then_inc(S.ldw, 16)
    V.wait_ge(S.ldx, 16)
    V.quantize_mx(T.q[:, xs * NC:(xs + 1) * NC], T.sc[:, xs * NC:(xs + 1) * NC], T.xb[:]).then_inc(S.qx, 1)
    V.wait_ge(S.ldw, 16)
    V.quantize_mx(T.q[:, 2 * NC:3 * NC], T.sc[:, 2 * NC:3 * NC], T.wb[:]).then_inc(S.qw, 1)
    tot.update(ldx=16, ldw=16, qx=1, qw=1)

    def put(kind, dsts, s0, d0s, ns, mask):
        _write(g, T, topo, core, dsts, _piece(T, kind, s0, ns), [_piece(T, kind, d, ns) for d in d0s], semx(me),
               mask, tot)

    g.wait_ge(S.qx, 1)
    if hub:
        partners = [at[(o, ch)] for o in P["outer_h"]]
        peers = [at[(h, rot(ch, 1))], at[(h, rot(ch, 2))]]
        for kind in "qs":
            put(kind, [cores[d] for d in peers], xs, [slot[d][("X", me)] for d in peers], 1, off)
        put("q", list(H["hq"]), xs, [0, 0], 1, up)
        put("s", [H["hs"]], xs, [0], 1, up)
    else:
        partner = at[(P["hub_h"], ch)]
        put("q", [H["hq"]], xs, [0], 1, up)
        put("s", [H["hs"]], xs, [0], 1, up)
        g.wait_ge(S.qw, 1)
        s0 = min(xs, 2)
        d0 = min(slot[partner][("X", me)], slot[partner][("W", me)])
        for kind in "qs":
            put(kind, [cores[partner]], s0, [d0], 2, off)
        put("q", [H["rq"]], xs, [0], 1, topo.mask(core, H["rq"]))
        put("s", [H["rs"]], xs, [0], 1, topo.mask(core, H["rs"]))
    nx = 2 * _ne(off)
    for j in range(N):
        if j != me:
            tot["X%d" % j] = nx

    w0, nw, own = (1, 3, NC) if hub else (2, 1, 0)
    TE.wait_ge(S.qx, 1)
    TE.wait_ge(S.qw, 1)
    if hub:
        for j in partners:
            TE.wait_ge(semx(j), nx)
    for k, j in enumerate(order):
        if j != me and not (hub and j in partners):
            TE.wait_ge(semx(j), nx)
        if k >= 8:
            TE.wait_ge(S.ev, 1)
        s = sl_me[("X", j)]
        bk = (k % 8) * 512
        TE.matmul_mx(T.zp[:, bk:bk + nw * NC], T.q[:, s * NC:(s + 1) * NC], T.sc[:, s * NC:(s + 1) * NC],
                     T.q[:, w0 * NC:(w0 + nw) * NC], T.sc[:, w0 * NC:(w0 + nw) * NC], True, True).then_inc(S.mm, 1)
    tot["mm"] = N

    def zsrc(j):
        k = pos[j]
        if k == 0:
            return T.ysb[:, j * NC:(j + 1) * NC]
        bk = (k % 8) * 512 + own
        return T.zp[:, bk:bk + NC]

    if hub:
        for k, j in enumerate(order):
            A.wait_ge(S.mm, k + 1)
            if k:
                A.wait_ge(S.sq, k)
            bk = (k % 8) * 512
            A.activation(T.junk[:], T.zp[:, bk:bk + nw * NC], ActivationFunctionType.Square,
                         accum_out=T.sp[:, col[j]:col[j] + 1]).then_inc(S.sq, 1)
        tot["sq"] = N
        hi = hubs.index(me)
        direct = peers + partners
        done = 0
        for b, js in enumerate(batches):
            done += len(js)
            g.wait_ge(S.sq, done)
            a0, a1 = LO[b], LO[b] + len(js)
            _write(g, T, topo, core, list(H["sm"]), T.sp[:, a0:a1], [T.sp[:, a0:a1] for d in H["sm"]],
                   S["S%d" % b], up, tot)
            _write(g, T, topo, core, [cores[d] for d in direct], T.sp[:, a0:a1],
                   [T.sl[:, hi * SW + a0:hi * SW + a1] for d in direct], S["S%d" % b], off, tot)
        V.wait_ge(S.sq, 1)
    else:
        V.wait_ge(S.mm, 1)
    V.tensor_copy(T.ysb[:, me * NC:(me + 1) * NC], T.zp[:, own:own + NC]).then_inc(S.ev, 1)
    tot["ev"] = 1

    c = {"vs": 0, "sa": 0, "zv": 0, "zs": 0, "st": 0, "st2": 0}

    def vop(inst):
        inst.then_inc(S.vs, 1)
        c["vs"] += 1

    def vsync():
        V.wait_ge(S.vs, c["vs"])

    def scale(eng, j):
        q = V if eng == "v" else A
        if pos[j] == 0:
            q.wait_ge(S.ev, 1)
        else:
            q.wait_ge(S.mm, pos[j] + 1)
        out = T.ysb[:, j * NC:(j + 1) * NC]
        rc = T.wk[:, 8 * SW + col[j]:8 * SW + col[j] + 1]
        if eng == "v":
            V.tensor_scalar(out, zsrc(j), rc, None, MUL).then_inc(S.zv, 1)
            c["zv"] += 1
        else:
            A.activation(out, zsrc(j), ActivationFunctionType.Copy, scale=rc).then_inc(S.zs, 1)
            c["zs"] += 1

    nrem = len([d for d in hubs if d != me])
    inv = 1.0 / (N * NC)
    done = 0
    for b, js in enumerate(batches):
        done += len(js)
        a0, a1 = LO[b], LO[b] + len(js)
        R = lambda k: T.wk[:, k * SW + a0:k * SW + a1]
        parts = [T.sp[:, a0:a1] if d == me else T.sl[:, i * SW + a0:i * SW + a1] for i, d in enumerate(hubs)]
        V.wait_ge(S["S%d" % b], _ne(off) * nrem)
        tot["S%d" % b] = _ne(off) * nrem
        if hub:
            V.wait_ge(S.sq, done)
        vop(V.tensor_tensor(R(0), parts[0], parts[1], ADD))
        vsync()
        vop(V.tensor_tensor(R(1), R(0), parts[2], ADD))
        A.wait_ge(S.vs, c["vs"])
        A.activation(R(3), R(1), ActivationFunctionType.Sqrt, bias=EPS, scale=inv).then_inc(S.sa, 1)
        c["sa"] += 1
        vsync()
        vop(V.tensor_scalar(R(2), R(1), inv, EPS, MUL, ADD))
        V.wait_ge(S.sa, c["sa"])
        vop(V.reciprocal(R(4), R(3)))
        vsync()
        vop(V.tensor_tensor(R(5), R(2), R(4), MUL))
        vsync()
        vop(V.tensor_tensor(R(6), R(5), R(4), MUL))
        vsync()
        vop(V.tensor_scalar(R(7), R(6), -0.5, 1.5, MUL, ADD))
        vsync()
        vop(V.tensor_tensor(R(8), R(4), R(7), MUL))
        vsync()
        A.wait_ge(S.vs, c["vs"])
        if b == 0:
            scale("v", js[0])
            scale("s", js[2])
            scale("v", js[1])
            SY.wait_ge(S.zv, c["zv"])
            SY.wait_ge(S.zs, c["zs"])
            SY.dma_start(T.y[:, js[0] * NC:(js[-1] + 1) * NC], T.ysb[:, js[0] * NC:(js[-1] + 1) * NC]).then_inc(S.st, 16)
            c["st"] += 16
        else:
            ga, gb = P["groups"][1], P["groups"][2]
            for j in ga:
                scale("v", j)
            for j in gb:
                scale("s", j)
            SY.wait_ge(S.zv, c["zv"])
            SY.dma_start(T.y[:, ga[0] * NC:(ga[-1] + 1) * NC], T.ysb[:, ga[0] * NC:(ga[-1] + 1) * NC]).then_inc(S.st, 16)
            c["st"] += 16
            A.wait_ge(S.zs, c["zs"])
            A.dma_start(T.y[:, gb[0] * NC:(gb[-1] + 1) * NC], T.ysb[:, gb[0] * NC:(gb[-1] + 1) * NC]).then_inc(S.st2, 16)
            c["st2"] += 16
    tot.update(c)

    for name in sorted(tot, key=lambda n: n in ("st", "st2")):
        g.wait_ge(S[name], tot[name])
